import numpy as np
import ml_dtypes


def mxq(x, axis, fmt="e4m3"):
    dtype, down = {"e4m3": (ml_dtypes.float8_e4m3fn, 7), "e5m2": (ml_dtypes.float8_e5m2, 14)}[fmt]
    v = np.moveaxis(np.asarray(x, np.float32).astype(ml_dtypes.bfloat16).astype(np.float64), axis, -1)
    blocks = v.reshape(v.shape[:-1] + (-1, 32))
    amax = np.abs(blocks).max(-1, keepdims=True)
    byte = np.maximum(np.where(amax > 0, np.frexp(amax)[1] - 1 + 127, 0) - down, 1)
    scale = np.exp2(byte - 127.0)
    codes = (blocks / scale).astype(np.float32).astype(dtype).astype(np.float64)
    return np.moveaxis((codes * scale).reshape(v.shape), -1, axis)


WIDE = False


def mx_kscale(k):
    if not WIDE:
        return np.ones(k)
    levels = np.array([30, -30])
    if k % 512:
        return np.exp2(np.random.permutation(np.resize(levels, k // 32))).repeat(32)
    a = np.empty((k // 512, 16))
    for p in range(k // 512):
        a[p, :8] = np.random.permutation(np.resize(levels, 8))
        for g in range(8):
            far = levels[np.abs(levels - a[p, g]) >= 10]
            a[p, g + 8] = far[np.random.randint(len(far))]
    return np.exp2(a.ravel()).repeat(32)


BF16 = ml_dtypes.bfloat16


def bf(x):
    return np.asarray(x, np.float32).astype(BF16)


def f64(x):
    return np.asarray(x).astype(np.float64)


E2M1 = np.array([0.0, 0.5, 1.0, 1.5, 2.0, 3.0, 4.0, 6.0, -0.0, -0.5, -1.0, -1.5, -2.0, -3.0, -4.0, -6.0])


def pack_weight(w, fmt):
    k, n = w.shape
    w = f64(bf(w)).reshape(k // 32, 32, n)
    amax = np.abs(w).max(1)
    if fmt == "e4m3":
        byte = np.frexp(amax)[1] - 1 + 127 - 7
    else:
        mant, ex = np.frexp(amax / 6.0)
        byte = np.where(mant > 0.5, ex, ex - 1) + 127
    byte = np.clip(np.where(amax > 0, byte, 1), 1, 254)
    scaled = (w * np.exp2(127.0 - byte)[:, None, :]).reshape(k, n).astype(np.float32)
    by_word = np.ascontiguousarray(scaled.reshape(k // 512, 128, 4, n).transpose(0, 1, 3, 2))
    if fmt == "e4m3":
        words = by_word.astype(ml_dtypes.float8_e4m3fn).view(np.uint8)
    else:
        c = by_word.astype(ml_dtypes.float4_e2m1fn).view(np.uint8) & 0xF
        words = c[..., 0::2] | (c[..., 1::2] << 4)
    return np.ascontiguousarray(words), np.ascontiguousarray(byte.astype(np.uint8).reshape(k // 512, 16, n))


def unpack_weight(words, scales, fmt):
    g, p, n, _ = words.shape
    if fmt == "e4m3":
        vals = np.ascontiguousarray(words).view(ml_dtypes.float8_e4m3fn).astype(np.float64)
    else:
        nib = np.empty((g, p, n, 4), np.uint8)
        nib[..., 0::2] = words & 0xF
        nib[..., 1::2] = words >> 4
        vals = E2M1[nib]
    vals = vals * np.repeat(np.exp2(scales.astype(np.float64) - 127.0), 8, axis=1)[..., None]
    return vals.transpose(0, 1, 3, 2).reshape(g * 512, n)
def pack4(w):
    words, scales = pack_weight(w, "e2m1")
    return words.reshape(words.shape[0], 128, -1), scales


def unpack4(words, scales):
    return unpack_weight(words.reshape(words.shape[0], 128, -1, 2), scales, "e2m1")


DOCS, K, F, R = 1024, 2048, 1024, 1024


def setup_inputs():
    s = mx_kscale(K)
    t = mx_kscale(DOCS)
    score = 1.5 * np.random.standard_normal(DOCS)
    diff = score[:, None] - score + 0.3 * np.random.standard_normal((DOCS, DOCS))
    w_words, w_scales = pack4(np.random.standard_normal((K, F)) / np.sqrt(K) / s[:, None])
    return {"x": bf(np.random.standard_normal((DOCS, K)) * s),
            "w_words": w_words,
            "w_scales": w_scales,
            "gain": bf(np.exp(0.7 * np.random.standard_normal(DOCS)) * t),
            "score": bf(score),
            "diff": bf(diff),
            "level": bf(np.random.uniform(-1, 1, R)),
            "prop": bf(8 * np.exp(0.3 * np.random.standard_normal(DOCS)) / np.sqrt(DOCS) / t)}


def reference(x, w_words, w_scales, gain, score, diff, level, prop):
    h = mxq(f64(x), 1, "e4m3") @ unpack4(w_words, w_scales)
    h = h * f64(gain)[:, None]
    spread = np.abs(f64(diff)).mean(1)
    perm = np.exp(f64(level)[:, None] * f64(score) - spread)
    perm = perm * f64(prop)
    return mxq(perm, 1, "e4m3") @ mxq(h, 0, "e5m2")

@@ -1,0 +1,389 @@
+from contextlib import ExitStack
+
+import concourse.mybir as mybir
+from concourse.masks import make_identity
+
+FLOPS = 2 * 1024 * 2048 * 1024 + 2 * 1024 * 1024 * 1024
+
+F32 = mybir.dt.float32
+BF16 = mybir.dt.bfloat16
+I32 = mybir.dt.int32
+U32 = mybir.dt.uint32
+U8 = mybir.dt.uint8
+E4M3 = mybir.dt.float8_e4m3fn_x4
+E5M2 = mybir.dt.float8_e5m2_x4
+E2M1 = mybir.dt.float4_e2m1fn_x4
+ALU = mybir.AluOpType
+ACT = mybir.ActivationFunctionType
+AXIS = mybir.AxisListType
+
+P = 128
+DOCS, K, F, R = 1024, 2048, 1024, 1024
+LN2 = 0.6931471805599453
+
+
+def tile_neuralsort_ranked_features_s9_kernel(tc, x, w_words, w_scales, gain, score, diff, level, prop, out):
+    nc = tc.nc
+    with ExitStack() as ctx:
+        keep = ctx.enter_context(tc.tile_pool(name="keep", bufs=1))
+        work = ctx.enter_context(tc.tile_pool(name="work", bufs=3))
+        outs = ctx.enter_context(tc.tile_pool(name="outs", bufs=16))
+        pa = ctx.enter_context(tc.psum_pool(name="pa", bufs=4))
+        pb = ctx.enter_context(tc.psum_pool(name="pb", bufs=4))
+        ctx.enter_context(tc.manual_schedule())
+
+        def kt(name, shape, dtype):
+            t = keep.tile(shape, dtype, name=name, align_bytes=64)
+            return t
+
+        x_view = x.rearrange("(g m t) k -> g t m k", g=2, t=4)
+        d_view = diff.rearrange("(g p t) l -> g p t l", g=2, t=4)
+        xr = [[kt("xr%d%d" % (g, t), [P, K], BF16) for t in range(4)] for g in range(2)]
+        xc = [[kt("xc%d%d" % (g, t), [P, 512], U32) for t in range(4)] for g in range(2)]
+        xs = [[kt("xs%d%d" % (g, t), [P, 512], U8) for t in range(4)] for g in range(2)]
+        wt = [kt("wt%d" % h, [P, 4, 1024], U8) for h in range(2)]
+        ws = kt("ws", [P, 4, 1024], U8)
+        dt = [kt("dt%d" % g, [P, 4, 1024], BF16) for g in range(2)]
+        hc = [[kt("hc%d%d" % (g, h), [P, 512], U32) for h in range(2)] for g in range(2)]
+        hs = [[kt("hs%d%d" % (g, h), [P, 512], U8) for h in range(2)] for g in range(2)]
+        hb = [[kt("hb%d%d" % (g, h), [P, 2048], BF16) for h in range(2)] for g in range(2)]
+        bc = [[kt("bc%d%d" % (g, h), [P, 512], U32) for h in range(2)] for g in range(2)]
+        bs = [[kt("bs%d%d" % (g, h), [P, 512], U8) for h in range(2)] for g in range(2)]
+        eb = [[kt("eb%d%d" % (g, h), [P, 4, 512], BF16) for h in range(2)] for g in range(2)]
+        bi = [[kt("bi%d%d" % (g, h), [P, 2048], BF16) for h in range(2)] for g in range(2)]
+        ident = kt("ident", [P, P], F32)
+        ones = kt("ones", [P, P], BF16)
+        one1 = kt("one1", [P, 1], F32)
+        dum = kt("dum", [P, 1], F32)
+        lrow = kt("lrow", [P, R], BF16)
+        lbc = kt("lbc", [P, R], BF16)
+        vg = kt("vg", [P, 8], BF16)
+        vs = kt("vs", [P, 8], BF16)
+        vp = kt("vp", [P, 8], BF16)
+        gp = kt("gp", [P, 8], F32)
+        s32 = kt("s32", [P, 8], F32)
+        p32 = kt("p32", [P, 8], F32)
+        expo = kt("expo", [P, 8], I32)
+        mant = kt("mant", [P, 8], I32)
+        elog = kt("elog", [P, 8], F32)
+        mlog = kt("mlog", [P, 8], F32)
+        plog = kt("plog", [P, 8], F32)
+        pos = kt("pos", [P, 8], F32)
+        nsg = kt("nsg", [P, 8], F32)
+        rs = kt("rs", [P, 8], F32)
+        cb = kt("cb", [P, 8], F32)
+
+        nc.vector.memset(one1[:], 1.0)
+        nc.vector.memset(ws[:].bitcast(I32), 0)
+        nc.vector.memset(lrow[:].bitcast(I32), 0)
+        nc.vector.memset(ones[:], 1.0)
+        make_identity(nc, ident[:])
+        nc.scalar.activation(out=dum[:], in_=one1[:], func=ACT.Ln)
+
+        ws_view = w_scales.bitcast(I32)
+        ww_view = w_words.bitcast(I32)
+
+        def load_scales():
+            for r in range(4):
+                nc.scalar.dma_start(
+                    out=ws[r:P:32, :, :].bitcast(I32),
+                    in_=ws_view[:, r:16:4, :].rearrange("c q n -> q c n"),
+                )
+
+        def load_x(g, t, h=None):
+            cols = slice(0, K) if h is None else slice(1024 * h, 1024 * h + 1024)
+            nc.sync.dma_start(out=xr[g][t][:, cols], in_=x_view[g, t][:, cols])
+
+        def load_w(h):
+            nc.sync.dma_start(
+                out=wt[h][:].bitcast(I32),
+                in_=ww_view[:, :, 256 * h:256 * h + 256].rearrange("c p n -> p c n"),
+            )
+
+        def load_d(g, half):
+            nc.sync.dma_start(out=dt[g][:, 2 * half:2 * half + 2, :], in_=d_view[g][:, 2 * half:2 * half + 2, :])
+
+        load_x(0, 0, 0)
+        load_x(0, 0, 1)
+        load_scales()
+        load_x(0, 1)
+        nc.scalar.dma_start(out=lrow[0:1, :], in_=level.rearrange("(o n) -> o n", o=1))
+        for v_tile, v in ((vp, prop), (vs, score), (vg, gain)):
+            nc.scalar.dma_start(
+                out=v_tile[:].rearrange("p (g t) -> p g t", t=4),
+                in_=v.rearrange("(g p t) -> p g t", g=2, t=4),
+            )
+        load_w(0)
+        load_x(0, 2)
+        load_d(0, 0)
+        load_x(0, 3)
+        load_d(0, 1)
+        load_x(1, 0)
+        load_x(1, 1)
+        load_w(1)
+        load_d(1, 0)
+        load_x(1, 2)
+        load_d(1, 1)
+        load_x(1, 3)
+
+        xg = {}
+        banks = {}
+        hbank = {}
+
+        def T(g, t):
+            words = xr[g][t][:].bitcast(F32)
+            for h in range(2):
+                ps = pa.tile([P, 512], F32, name="pa")
+                banks[g, t, h] = ps
+                for c in range(2):
+                    for u in range(2):
+                        a = 256 * (2 * h + c)
+                        nc.tensor.transpose(
+                            ps[:, 256 * c + 128 * u:256 * c + 128 * u + 128],
+                            words[:, a + u:a + 256:2],
+                            ident[:],
+                        )
+
+        def Xc(g, t):
+            tile = work.tile([P, K], BF16, name="xg", align_bytes=64)
+            xg[g, t] = tile
+            for h in range(2):
+                ps = banks[g, t, h]
+                nc.scalar.copy(
+                    out=tile[:].bitcast(F32)[:, 512 * h:512 * h + 512].rearrange("p (c m u) -> p c m u", c=2, u=2),
+                    in_=ps[:].rearrange("p (c u m) -> p c m u", c=2, u=2),
+                )
+
+        def Xq(g, t):
+            nc.vector.quantize_mx(out=xc[g][t][:].bitcast(E4M3), scales=xs[g][t][:], in_=xg[g, t][:])
+
+        def S1(g, t, fb):
+            if (g, fb) not in hbank:
+                hps = pb.tile([P, 512], F32, name="pb")
+                hbank[g, fb] = hps
+            h, b = divmod(fb, 4)
+            for c in range(4):
+                nc.tensor.matmul_mx(
+                    out=hbank[g, fb][:, 128 * t:128 * t + 128],
+                    lhsT=xc[g][t][:, 128 * c:128 * c + 128].bitcast(E4M3),
+                    lhsT_scale=xs[g][t][:, 128 * c:128 * c + 128],
+                    rhs=wt[h][:, c, 256 * b:256 * b + 256].bitcast(E2M1),
+                    rhs_scale=ws[:, c, 128 * fb:128 * fb + 128],
+                    start=(c == 0),
+                    stop=(c == 3),
+                )
+
+        def Hc(g, fb):
+            h, b = divmod(fb, 4)
+            nc.vector.tensor_tensor(
+                out=hb[g][h][:, 512 * b:512 * b + 512].rearrange("p (f t) -> p f t", t=4),
+                in0=hbank[g, fb][:].rearrange("p (t f) -> p f t", t=4),
+                in1=gp[:, 4 * g:4 * g + 4].unsqueeze(1).to_broadcast([P, P, 4]),
+                op=ALU.mult,
+            )
+
+        def Hq(g, h, half):
+            w = slice(256 * half, 256 * half + 256)
+            nc.vector.quantize_mx(
+                out=hc[g][h][:, w].bitcast(E5M2),
+                scales=hs[g][h][:, w],
+                in_=hb[g][h][:, 1024 * half:1024 * half + 1024],
+            )
+
+        def Dv(g, t):
+            nc.vector.tensor_reduce(
+                out=rs[:, 4 * g + t:4 * g + t + 1], in_=dt[g][:, t, :], axis=AXIS.X, op=ALU.add,
+                apply_absolute_value=True,
+            )
+
+        def Ds(g, t):
+            junk = work.tile([P, 1024], BF16, name="junk")
+            nc.scalar.activation(
+                out=junk[:], in_=dt[g][:, t, :], func=ACT.Abs, accum_out=rs[:, 4 * g + t:4 * g + t + 1])
+
+        def Cb(g):
+            w = slice(4 * g, 4 * g + 4)
+            nc.vector.scalar_tensor_tensor(
+                out=cb[:, w], in0=rs[:, w], scalar=-1.0 / 1024.0, in1=plog[:, w], op0=ALU.mult, op1=ALU.add)
+
+        def E(g, h, t):
+            j = 4 * g + t
+            nc.scalar.activation(
+                out=eb[g][h][:, t, :], in_=lbc[:, 512 * h:512 * h + 512], func=ACT.Exp,
+                bias=cb[:, j:j + 1], scale=s32[:, j:j + 1])
+
+        def Bi(g, h):
+            nc.vector.tensor_copy(
+                out=bi[g][h][:].rearrange("p (i t) -> p i t", t=4),
+                in_=eb[g][h][:].rearrange("p t i -> p i t"),
+            )
+
+        def Bq(g, h):
+            nc.vector.quantize_mx(out=bc[g][h][:].bitcast(E4M3), scales=bs[g][h][:], in_=bi[g][h][:])
+
+        obank = {}
+
+        def S2(i, f):
+            pool, nm = ((pa, "pa"), (pb, "pb"))[len(obank) % 2]
+            ops = pool.tile([P, 512], F32, name=nm)
+            obank[i, f] = ops
+            h, b = divmod(i, 4)
+            for g in range(2):
+                nc.tensor.matmul_mx(
+                    out=ops[:],
+                    lhsT=bc[g][h][:, 128 * b:128 * b + 128].bitcast(E4M3),
+                    lhsT_scale=bs[g][h][:, 128 * b:128 * b + 128],
+                    rhs=hc[g][f][:].bitcast(E5M2),
+                    rhs_scale=hs[g][f][:],
+                    start=(g == 0),
+                    stop=(g == 1),
+                )
+
+        def O(i, f, eng):
+            ot = outs.tile([P, 512], F32, name="ot")
+            if eng == 0:
+                nc.vector.tensor_copy(out=ot[:], in_=obank[i, f][:])
+            else:
+                nc.scalar.copy(out=ot[:], in_=obank[i, f][:])
+            nc.sync.dma_start(out=out[128 * i:128 * i + 128, 512 * f:512 * f + 512], in_=ot[:])
+
+        def vectors():
+            nc.vector.tensor_copy(out=p32[:], in_=vp[:])
+            nc.vector.tensor_scalar(
+                out=expo[:], in0=p32[:].bitcast(I32), scalar1=23, scalar2=255,
+                op0=ALU.logical_shift_right, op1=ALU.bitwise_and)
+            nc.vector.tensor_scalar(
+                out=mant[:], in0=p32[:].bitcast(I32), scalar1=0x7FFFFF, scalar2=0x3F800000,
+                op0=ALU.bitwise_and, op1=ALU.bitwise_or)
+            nc.vector.tensor_copy(out=s32[:], in_=vs[:])
+            nc.vector.tensor_scalar(
+                out=elog[:], in0=expo[:], scalar1=127.0, scalar2=LN2, op0=ALU.subtract, op1=ALU.mult)
+            nc.vector.tensor_scalar(
+                out=pos[:], in0=p32[:], scalar1=0.0, scalar2=None, op0=ALU.is_gt)
+            nc.vector.scalar_tensor_tensor(
+                out=nsg[:], in0=p32[:], scalar=0.0, in1=pos[:], op0=ALU.is_lt, op1=ALU.subtract)
+            nc.vector.scalar_tensor_tensor(
+                out=gp[:], in0=nsg[:], scalar=-1.0, in1=vg[:], op0=ALU.mult, op1=ALU.mult)
+
+        T(0, 0)
+        lps = [pb.tile([P, 512], F32, name="pb") for n in range(2)]
+        for n in range(2):
+            nc.tensor.matmul(lps[n][:], lhsT=ones[:], rhs=lrow[:, 512 * n:512 * n + 512], start=True, stop=True)
+        Xc(0, 0)
+        Xq(0, 0)
+        for n in range(2):
+            nc.vector.tensor_copy(out=lbc[:, 512 * n:512 * n + 512], in_=lps[n][:])
+        T(0, 1)
+        vectors()
+        Xc(0, 1)
+        Xq(0, 1)
+        nc.scalar.activation(out=mlog[:], in_=mant[:].bitcast(F32), func=ACT.Ln)
+        nc.scalar.activation(out=dum[:], in_=one1[:], func=ACT.Exp)
+        nc.vector.tensor_tensor(out=plog[:], in0=mlog[:], in1=elog[:], op=ALU.add)
+        for fb in range(4):
+            S1(0, 0, fb)
+        T(0, 2)
+        Xc(0, 2)
+        Dv(0, 0)
+        Xq(0, 2)
+        for fb in range(4):
+            S1(0, 1, fb)
+        T(0, 3)
+        Ds(0, 1)
+        Xc(0, 3)
+        Dv(0, 2)
+        Xq(0, 3)
+        Ds(0, 3)
+        for fb in range(4):
+            S1(0, 2, fb)
+        T(1, 0)
+        Cb(0)
+        Xc(1, 0)
+        E(0, 0, 0)
+        for fb in range(4):
+            S1(0, 3, fb)
+            Hc(0, fb)
+            if fb == 1:
+                Xq(1, 0)
+
+        def S1all(g, fb):
+            for t in range(4):
+                S1(g, t, fb)
+
+        T(1, 1)
+        E(0, 0, 1)
+        Xc(1, 1)
+        E(0, 0, 2)
+        E(0, 0, 3)
+        Hq(0, 0, 0)
+        S1all(0, 4)
+        Hq(0, 0, 1)
+        Xq(1, 1)
+        Hc(0, 4)
+        T(1, 2)
+        Xc(1, 2)
+        Ds(1, 0)
+        S1all(0, 5)
+        Bi(0, 0)
+        Xq(1, 2)
+        Hc(0, 5)
+        T(1, 3)
+        Xc(1, 3)
+        Ds(1, 1)
+        Hq(0, 1, 0)
+        Bq(0, 0)
+        S1all(0, 6)
+        Xq(1, 3)
+        Hc(0, 6)
+        S1all(0, 7)
+        Ds(1, 2)
+        Dv(1, 3)
+        Hc(0, 7)
+        Cb(1)
+
+        for t in range(4):
+            E(1, 0, t)
+        S1all(1, 0)
+        Hq(0, 1, 1)
+        Hc(1, 0)
+        S1all(1, 1)
+        Hc(1, 1)
+        for t in range(4):
+            E(0, 1, t)
+        S1all(1, 2)
+        Hq(1, 0, 0)
+        Hc(1, 2)
+        Bi(1, 0)
+        S1all(1, 3)
+        Hc(1, 3)
+        Bq(1, 0)
+        for t in range(4):
+            E(1, 1, t)
+        S1all(1, 4)
+        Hq(1, 0, 1)
+        Hc(1, 4)
+        S1all(1, 5)
+        Hc(1, 5)
+        S1all(1, 6)
+        Hq(1, 1, 0)
+        Hc(1, 6)
+        S1all(1, 7)
+        Hc(1, 7)
+
+        for i in range(4):
+            S2(i, 0)
+            if i == 0:
+                Bi(0, 1)
+                Hq(1, 1, 1)
+                Bi(1, 1)
+                Bq(0, 1)
+                Bq(1, 1)
+            O(i, 0, 1)
+        for i in range(4):
+            S2(i, 1)
+            O(i, 1, 1)
+        for i in range(4, 8):
+            S2(i, 0)
+            O(i, 0, i % 2)
+            S2(i, 1)
+            O(i, 1, 1 - i % 2)

@@ -78,8 +78,6 @@ def tile_neuralsort_ranked_features_s9_kernel(tc, x, w_words, w_scales, gain, sc
         nc.vector.memset(lrow[:].bitcast(I32), 0)
         nc.vector.memset(ones[:], 1.0)
         make_identity(nc, ident[:])
-        nc.scalar.activation(out=dum[:], in_=one1[:], func=ACT.Ln)
-
         ws_view = w_scales.bitcast(I32)
         ww_view = w_words.bitcast(I32)
 
@@ -103,18 +101,23 @@ def tile_neuralsort_ranked_features_s9_kernel(tc, x, w_words, w_scales, gain, sc
         def load_d(g, half):
             nc.sync.dma_start(out=dt[g][:, 2 * half:2 * half + 2, :], in_=d_view[g][:, 2 * half:2 * half + 2, :])
 
-        load_x(0, 0, 0)
-        load_x(0, 0, 1)
-        load_scales()
-        load_x(0, 1)
-        nc.scalar.dma_start(out=lrow[0:1, :], in_=level.rearrange("(o n) -> o n", o=1))
-        for v_tile, v in ((vp, prop), (vs, score), (vg, gain)):
-            nc.scalar.dma_start(
+        def load_vec(eng, v_tile, v):
+            eng.dma_start(
                 out=v_tile[:].rearrange("p (g t) -> p g t", t=4),
                 in_=v.rearrange("(g p t) -> p g t", g=2, t=4),
             )
+
+        load_vec(nc.scalar, vp, prop)
+        load_x(0, 0, 0)
+        load_x(0, 0, 1)
+        load_scales()
+        nc.scalar.activation(out=dum[:], in_=one1[:], func=ACT.Ln)
+        load_x(0, 1)
         load_w(0)
         load_x(0, 2)
+        load_vec(nc.sync, vs, score)
+        load_vec(nc.sync, vg, gain)
+        nc.sync.dma_start(out=lrow[0:1, :], in_=level.rearrange("(o n) -> o n", o=1))
         load_d(0, 0)
         load_x(0, 3)
         load_d(0, 1)
@@ -214,8 +217,8 @@ def tile_neuralsort_ranked_features_s9_kernel(tc, x, w_words, w_scales, gain, sc
 
         def Bi(g, h):
             nc.vector.tensor_copy(
-                out=bi[g][h][:].rearrange("p (i t) -> p i t", t=4),
-                in_=eb[g][h][:].rearrange("p t i -> p i t"),
+                out=bi[g][h][:].rearrange("p (c i t) -> p c t i", i=4, t=4),
+                in_=eb[g][h][:].rearrange("p t (c i) -> p c t i", i=4),
             )
 
         def Bq(g, h):
@@ -223,21 +226,27 @@ def tile_neuralsort_ranked_features_s9_kernel(tc, x, w_words, w_scales, gain, sc
 
         obank = {}
 
-        def S2(i, f):
-            pool, nm = ((pa, "pa"), (pb, "pb"))[len(obank) % 2]
+        def S2g(i, f, g):
+            h, b = divmod(i, 4)
+            nc.tensor.matmul_mx(
+                out=obank[i, f][:],
+                lhsT=bc[g][h][:, 128 * b:128 * b + 128].bitcast(E4M3),
+                lhsT_scale=bs[g][h][:, 128 * b:128 * b + 128],
+                rhs=hc[g][f][:].bitcast(E5M2),
+                rhs_scale=hs[g][f][:],
+                start=(g == 0),
+                stop=(g == 1),
+            )
+
+        def S2t(i, f):
+            pool, nm = ((pa, "pa"), (pb, "pb"))[f if i < 4 else len(obank) % 2]
             ops = pool.tile([P, 512], F32, name=nm)
             obank[i, f] = ops
-            h, b = divmod(i, 4)
-            for g in range(2):
-                nc.tensor.matmul_mx(
-                    out=ops[:],
-                    lhsT=bc[g][h][:, 128 * b:128 * b + 128].bitcast(E4M3),
-                    lhsT_scale=bs[g][h][:, 128 * b:128 * b + 128],
-                    rhs=hc[g][f][:].bitcast(E5M2),
-                    rhs_scale=hs[g][f][:],
-                    start=(g == 0),
-                    stop=(g == 1),
-                )
+
+        def S2(i, f):
+            S2t(i, f)
+            S2g(i, f, 0)
+            S2g(i, f, 1)
 
         def O(i, f, eng):
             ot = outs.tile([P, 512], F32, name="ot")
@@ -255,31 +264,28 @@ def tile_neuralsort_ranked_features_s9_kernel(tc, x, w_words, w_scales, gain, sc
             nc.vector.tensor_scalar(
                 out=mant[:], in0=p32[:].bitcast(I32), scalar1=0x7FFFFF, scalar2=0x3F800000,
                 op0=ALU.bitwise_and, op1=ALU.bitwise_or)
-            nc.vector.tensor_copy(out=s32[:], in_=vs[:])
             nc.vector.tensor_scalar(
                 out=elog[:], in0=expo[:], scalar1=127.0, scalar2=LN2, op0=ALU.subtract, op1=ALU.mult)
             nc.vector.tensor_scalar(
                 out=pos[:], in0=p32[:], scalar1=0.0, scalar2=None, op0=ALU.is_gt)
             nc.vector.scalar_tensor_tensor(
                 out=nsg[:], in0=p32[:], scalar=0.0, in1=pos[:], op0=ALU.is_lt, op1=ALU.subtract)
+
+        def vectors2():
+            nc.vector.tensor_copy(out=s32[:], in_=vs[:])
             nc.vector.scalar_tensor_tensor(
                 out=gp[:], in0=nsg[:], scalar=-1.0, in1=vg[:], op0=ALU.mult, op1=ALU.mult)
 
-        T(0, 0)
-        lps = [pb.tile([P, 512], F32, name="pb") for n in range(2)]
-        for n in range(2):
-            nc.tensor.matmul(lps[n][:], lhsT=ones[:], rhs=lrow[:, 512 * n:512 * n + 512], start=True, stop=True)
-        Xc(0, 0)
-        Xq(0, 0)
-        for n in range(2):
-            nc.vector.tensor_copy(out=lbc[:, 512 * n:512 * n + 512], in_=lps[n][:])
-        T(0, 1)
         vectors()
+        nc.scalar.activation(out=mlog[:], in_=mant[:].bitcast(F32), func=ACT.Ln)
+        nc.vector.tensor_tensor(out=plog[:], in0=mlog[:], in1=elog[:], op=ALU.add)
+        T(0, 0)
+        Xc(0, 0)
+        nc.scalar.activation(out=dum[:], in_=one1[:], func=ACT.Exp)
+        Xq(0, 0)
+        T(0, 1)
         Xc(0, 1)
         Xq(0, 1)
-        nc.scalar.activation(out=mlog[:], in_=mant[:].bitcast(F32), func=ACT.Ln)
-        nc.scalar.activation(out=dum[:], in_=one1[:], func=ACT.Exp)
-        nc.vector.tensor_tensor(out=plog[:], in0=mlog[:], in1=elog[:], op=ALU.add)
         for fb in range(4):
             S1(0, 0, fb)
         T(0, 2)
@@ -288,6 +294,12 @@ def tile_neuralsort_ranked_features_s9_kernel(tc, x, w_words, w_scales, gain, sc
         Xq(0, 2)
         for fb in range(4):
             S1(0, 1, fb)
+        vectors2()
+        lps = [pa.tile([P, 512], F32, name="pa") for n in range(2)]
+        for n in range(2):
+            nc.tensor.matmul(lps[n][:], lhsT=ones[:], rhs=lrow[:, 512 * n:512 * n + 512], start=True, stop=True)
+        for n in range(2):
+            nc.vector.tensor_copy(out=lbc[:, 512 * n:512 * n + 512], in_=lps[n][:])
         T(0, 3)
         Ds(0, 1)
         Xc(0, 3)
@@ -337,18 +349,19 @@ def tile_neuralsort_ranked_features_s9_kernel(tc, x, w_words, w_scales, gain, sc
         Hc(0, 6)
         S1all(0, 7)
         Ds(1, 2)
-        Dv(1, 3)
+        Ds(1, 3)
         Hc(0, 7)
         Cb(1)
 
-        for t in range(4):
-            E(1, 0, t)
+        E(0, 1, 0)
         S1all(1, 0)
         Hq(0, 1, 1)
         Hc(1, 0)
+        for t in range(4):
+            E(1, 0, t)
         S1all(1, 1)
         Hc(1, 1)
-        for t in range(4):
+        for t in range(1, 4):
             E(0, 1, t)
         S1all(1, 2)
         Hq(1, 0, 0)
@@ -357,30 +370,35 @@ def tile_neuralsort_ranked_features_s9_kernel(tc, x, w_words, w_scales, gain, sc
         S1all(1, 3)
         Hc(1, 3)
         Bq(1, 0)
+        Hq(1, 0, 1)
         for t in range(4):
             E(1, 1, t)
         S1all(1, 4)
-        Hq(1, 0, 1)
         Hc(1, 4)
         S1all(1, 5)
         Hc(1, 5)
+        for i in range(2):
+            S2(i, 0)
+            O(i, 0, 1)
         S1all(1, 6)
         Hq(1, 1, 0)
         Hc(1, 6)
+        for i in range(2, 4):
+            S2(i, 0)
+            O(i, 0, 1)
         S1all(1, 7)
+        Bi(0, 1)
         Hc(1, 7)
+        Bq(0, 1)
+        Hq(1, 1, 1)
+        Bi(1, 1)
+        Bq(1, 1)
 
         for i in range(4):
-            S2(i, 0)
-            if i == 0:
-                Bi(0, 1)
-                Hq(1, 1, 1)
-                Bi(1, 1)
-                Bq(0, 1)
-                Bq(1, 1)
-            O(i, 0, 1)
+            S2t(i, 1)
+            S2g(i, 1, 0)
         for i in range(4):
-            S2(i, 1)
+            S2g(i, 1, 1)
             O(i, 1, 1)
         for i in range(4, 8):
             S2(i, 0)

@@ -42,7 +42,7 @@ def tile_neuralsort_ranked_features_s9_kernel(tc, x, w_words, w_scales, gain, sc
         xc = [[kt("xc%d%d" % (g, t), [P, 512], U32) for t in range(4)] for g in range(2)]
         xs = [[kt("xs%d%d" % (g, t), [P, 512], U8) for t in range(4)] for g in range(2)]
         wt = [kt("wt%d" % h, [P, 4, 1024], U8) for h in range(2)]
-        ws = kt("ws", [P, 4, 1024], U8)
+        ws = [kt("ws%d" % h, [P, 4, 512], U8) for h in range(2)]
         dt = [kt("dt%d" % g, [P, 4, 1024], BF16) for g in range(2)]
         hc = [[kt("hc%d%d" % (g, h), [P, 512], U32) for h in range(2)] for g in range(2)]
         hs = [[kt("hs%d%d" % (g, h), [P, 512], U8) for h in range(2)] for g in range(2)]
@@ -56,6 +56,7 @@ def tile_neuralsort_ranked_features_s9_kernel(tc, x, w_words, w_scales, gain, sc
         one1 = kt("one1", [P, 1], F32)
         dum = kt("dum", [P, 1], F32)
         lrow = kt("lrow", [P, R], BF16)
+        zeros = kt("zeros", [P, 512], BF16)
         lbc = kt("lbc", [P, R], BF16)
         vg = kt("vg", [P, 8], BF16)
         vs = kt("vs", [P, 8], BF16)
@@ -74,18 +75,20 @@ def tile_neuralsort_ranked_features_s9_kernel(tc, x, w_words, w_scales, gain, sc
         cb = kt("cb", [P, 8], F32)
 
         nc.vector.memset(one1[:], 1.0)
-        nc.vector.memset(ws[:].bitcast(I32), 0)
+        nc.vector.memset(ws[0][:].bitcast(I32), 0)
         nc.vector.memset(lrow[:].bitcast(I32), 0)
         nc.vector.memset(ones[:], 1.0)
         make_identity(nc, ident[:])
+        nc.gpsimd.memset(zeros[:].bitcast(I32), 0)
+        nc.gpsimd.memset(ws[1][:].bitcast(I32), 0)
         ws_view = w_scales.bitcast(I32)
         ww_view = w_words.bitcast(I32)
 
-        def load_scales():
+        def load_scales(eng, h):
             for r in range(4):
-                nc.scalar.dma_start(
-                    out=ws[r:P:32, :, :].bitcast(I32),
-                    in_=ws_view[:, r:16:4, :].rearrange("c q n -> q c n"),
+                eng.dma_start(
+                    out=ws[h][r:P:32, :, :].bitcast(I32),
+                    in_=ws_view[:, r:16:4, 128 * h:128 * h + 128].rearrange("c q n -> q c n"),
                 )
 
         def load_x(g, t, h=None):
@@ -109,8 +112,8 @@ def tile_neuralsort_ranked_features_s9_kernel(tc, x, w_words, w_scales, gain, sc
 
         load_vec(nc.scalar, vp, prop)
         load_x(0, 0, 0)
+        load_scales(nc.sync, 0)
         load_x(0, 0, 1)
-        load_scales()
         nc.scalar.activation(out=dum[:], in_=one1[:], func=ACT.Ln)
         load_x(0, 1)
         load_w(0)
@@ -123,11 +126,12 @@ def tile_neuralsort_ranked_features_s9_kernel(tc, x, w_words, w_scales, gain, sc
         load_d(0, 1)
         load_x(1, 0)
         load_x(1, 1)
+        load_scales(nc.sync, 1)
         load_w(1)
-        load_d(1, 0)
         load_x(1, 2)
-        load_d(1, 1)
         load_x(1, 3)
+        load_d(1, 0)
+        load_d(1, 1)
 
         xg = {}
         banks = {}
@@ -171,7 +175,7 @@ def tile_neuralsort_ranked_features_s9_kernel(tc, x, w_words, w_scales, gain, sc
                     lhsT=xc[g][t][:, 128 * c:128 * c + 128].bitcast(E4M3),
                     lhsT_scale=xs[g][t][:, 128 * c:128 * c + 128],
                     rhs=wt[h][:, c, 256 * b:256 * b + 256].bitcast(E2M1),
-                    rhs_scale=ws[:, c, 128 * fb:128 * fb + 128],
+                    rhs_scale=ws[h][:, c, 128 * b:128 * b + 128],
                     start=(c == 0),
                     stop=(c == 3),
                 )
@@ -215,8 +219,8 @@ def tile_neuralsort_ranked_features_s9_kernel(tc, x, w_words, w_scales, gain, sc
                 out=eb[g][h][:, t, :], in_=lbc[:, 512 * h:512 * h + 512], func=ACT.Exp,
                 bias=cb[:, j:j + 1], scale=s32[:, j:j + 1])
 
-        def Bi(g, h):
-            nc.vector.tensor_copy(
+        def Bi(g, h, copy=nc.vector.tensor_copy):
+            copy(
                 out=bi[g][h][:].rearrange("p (c i t) -> p c t i", i=4, t=4),
                 in_=eb[g][h][:].rearrange("p t (c i) -> p c t i", i=4),
             )
@@ -239,7 +243,7 @@ def tile_neuralsort_ranked_features_s9_kernel(tc, x, w_words, w_scales, gain, sc
             )
 
         def S2t(i, f):
-            pool, nm = ((pa, "pa"), (pb, "pb"))[f if i < 4 else len(obank) % 2]
+            pool, nm = ((pa, "pa"), (pb, "pb"))[f]
             ops = pool.tile([P, 512], F32, name=nm)
             obank[i, f] = ops
 
@@ -248,7 +252,21 @@ def tile_neuralsort_ranked_features_s9_kernel(tc, x, w_words, w_scales, gain, sc
             S2g(i, f, 0)
             S2g(i, f, 1)
 
+        joined = {}
+
         def O(i, f, eng):
+            if 4 <= i < 7:
+                if i not in joined:
+                    pair = outs.tile([P, 1024], F32, name="pair", bufs=3)
+                    joined[i] = pair
+                half = joined[i][:, 512 * f:512 * f + 512]
+                if eng == 0:
+                    nc.vector.tensor_copy(out=half, in_=obank[i, f][:])
+                else:
+                    nc.scalar.copy(out=half, in_=obank[i, f][:])
+                if f == 1:
+                    nc.sync.dma_start(out=out[128 * i:128 * i + 128, :], in_=joined[i][:])
+                return
             ot = outs.tile([P, 512], F32, name="ot")
             if eng == 0:
                 nc.vector.tensor_copy(out=ot[:], in_=obank[i, f][:])
@@ -276,12 +294,15 @@ def tile_neuralsort_ranked_features_s9_kernel(tc, x, w_words, w_scales, gain, sc
             nc.vector.scalar_tensor_tensor(
                 out=gp[:], in0=nsg[:], scalar=-1.0, in1=vg[:], op0=ALU.mult, op1=ALU.mult)
 
+        warm = pb.tile([P, 512], F32, name="pb")
+        for n in range(4):
+            nc.tensor.matmul(warm[:], lhsT=ones[:], rhs=zeros[:], start=True, stop=True)
         vectors()
         nc.scalar.activation(out=mlog[:], in_=mant[:].bitcast(F32), func=ACT.Ln)
         nc.vector.tensor_tensor(out=plog[:], in0=mlog[:], in1=elog[:], op=ALU.add)
+        nc.scalar.activation(out=dum[:], in_=one1[:], func=ACT.Exp)
         T(0, 0)
         Xc(0, 0)
-        nc.scalar.activation(out=dum[:], in_=one1[:], func=ACT.Exp)
         Xq(0, 0)
         T(0, 1)
         Xc(0, 1)
@@ -334,19 +355,19 @@ def tile_neuralsort_ranked_features_s9_kernel(tc, x, w_words, w_scales, gain, sc
         Hc(0, 4)
         T(1, 2)
         Xc(1, 2)
-        Ds(1, 0)
-        S1all(0, 5)
-        Bi(0, 0)
-        Xq(1, 2)
-        Hc(0, 5)
         T(1, 3)
         Xc(1, 3)
-        Ds(1, 1)
+        Bi(0, 0)
+        S1all(0, 5)
+        Xq(1, 2)
+        Hc(0, 5)
+        Ds(1, 0)
         Hq(0, 1, 0)
+        Xq(1, 3)
         Bq(0, 0)
         S1all(0, 6)
-        Xq(1, 3)
         Hc(0, 6)
+        Ds(1, 1)
         S1all(0, 7)
         Ds(1, 2)
         Ds(1, 3)
@@ -377,21 +398,21 @@ def tile_neuralsort_ranked_features_s9_kernel(tc, x, w_words, w_scales, gain, sc
         Hc(1, 4)
         S1all(1, 5)
         Hc(1, 5)
+        Bi(0, 1)
+        S1all(1, 6)
         for i in range(2):
             S2(i, 0)
             O(i, 0, 1)
-        S1all(1, 6)
-        Hq(1, 1, 0)
         Hc(1, 6)
+        Hq(1, 1, 0)
+        S1all(1, 7)
+        Bi(1, 1, nc.scalar.copy)
+        Bq(0, 1)
+        Hc(1, 7)
         for i in range(2, 4):
             S2(i, 0)
             O(i, 0, 1)
-        S1all(1, 7)
-        Bi(0, 1)
-        Hc(1, 7)
-        Bq(0, 1)
         Hq(1, 1, 1)
-        Bi(1, 1)
         Bq(1, 1)
 
         for i in range(4):
@@ -399,7 +420,7 @@ def tile_neuralsort_ranked_features_s9_kernel(tc, x, w_words, w_scales, gain, sc
             S2g(i, 1, 0)
         for i in range(4):
             S2g(i, 1, 1)
-            O(i, 1, 1)
+            O(i, 1, i % 2)
         for i in range(4, 8):
             S2(i, 0)
             O(i, 0, i % 2)

@@ -56,7 +56,6 @@ def tile_neuralsort_ranked_features_s9_kernel(tc, x, w_words, w_scales, gain, sc
         one1 = kt("one1", [P, 1], F32)
         dum = kt("dum", [P, 1], F32)
         lrow = kt("lrow", [P, R], BF16)
-        zeros = kt("zeros", [P, 512], BF16)
         lbc = kt("lbc", [P, R], BF16)
         vg = kt("vg", [P, 8], BF16)
         vs = kt("vs", [P, 8], BF16)
@@ -75,12 +74,12 @@ def tile_neuralsort_ranked_features_s9_kernel(tc, x, w_words, w_scales, gain, sc
         cb = kt("cb", [P, 8], F32)
 
         nc.vector.memset(one1[:], 1.0)
-        nc.vector.memset(ws[0][:].bitcast(I32), 0)
-        nc.vector.memset(lrow[:].bitcast(I32), 0)
         nc.vector.memset(ones[:], 1.0)
+        nc.vector.memset(lrow[:].bitcast(I32), 0)
+        nc.vector.memset(ws[0][:].bitcast(I32), 0)
         make_identity(nc, ident[:])
-        nc.gpsimd.memset(zeros[:].bitcast(I32), 0)
         nc.gpsimd.memset(ws[1][:].bitcast(I32), 0)
+
         ws_view = w_scales.bitcast(I32)
         ww_view = w_words.bitcast(I32)
 
@@ -111,16 +110,15 @@ def tile_neuralsort_ranked_features_s9_kernel(tc, x, w_words, w_scales, gain, sc
             )
 
         load_vec(nc.scalar, vp, prop)
-        load_x(0, 0, 0)
-        load_scales(nc.sync, 0)
-        load_x(0, 0, 1)
+        nc.scalar.dma_start(out=lrow[0:1, :], in_=level.rearrange("(o n) -> o n", o=1))
+        load_x(0, 0)
         nc.scalar.activation(out=dum[:], in_=one1[:], func=ACT.Ln)
         load_x(0, 1)
+        load_scales(nc.sync, 0)
         load_w(0)
         load_x(0, 2)
         load_vec(nc.sync, vs, score)
         load_vec(nc.sync, vg, gain)
-        nc.sync.dma_start(out=lrow[0:1, :], in_=level.rearrange("(o n) -> o n", o=1))
         load_d(0, 0)
         load_x(0, 3)
         load_d(0, 1)
@@ -137,8 +135,21 @@ def tile_neuralsort_ranked_features_s9_kernel(tc, x, w_words, w_scales, gain, sc
         banks = {}
         hbank = {}
 
+        sorted_words = {}
+
+        def Wsort(g, t):
+            tile = work.tile([P, 1024], F32, name="xw", align_bytes=64)
+            sorted_words[g, t] = tile
+            for h in range(2):
+                w = slice(512 * h, 512 * h + 512)
+                nc.vector.tensor_copy(
+                    out=tile[:, w].rearrange("p (c u q) -> p c u q", c=2, u=2),
+                    in_=xr[g][t][:].bitcast(F32)[:, w].rearrange("p (c q u) -> p c u q", c=2, u=2),
+                )
+
         def T(g, t):
-            words = xr[g][t][:].bitcast(F32)
+            swd = sorted_words.get((g, t))
+            words = xr[g][t][:].bitcast(F32) if swd is None else swd[:]
             for h in range(2):
                 ps = pa.tile([P, 512], F32, name="pa")
                 banks[g, t, h] = ps
@@ -147,7 +158,7 @@ def tile_neuralsort_ranked_features_s9_kernel(tc, x, w_words, w_scales, gain, sc
                         a = 256 * (2 * h + c)
                         nc.tensor.transpose(
                             ps[:, 256 * c + 128 * u:256 * c + 128 * u + 128],
-                            words[:, a + u:a + 256:2],
+                            words[:, a + u:a + 256:2] if swd is None else words[:, a + 128 * u:a + 128 * u + 128],
                             ident[:],
                         )
 
@@ -219,10 +230,10 @@ def tile_neuralsort_ranked_features_s9_kernel(tc, x, w_words, w_scales, gain, sc
                 out=eb[g][h][:, t, :], in_=lbc[:, 512 * h:512 * h + 512], func=ACT.Exp,
                 bias=cb[:, j:j + 1], scale=s32[:, j:j + 1])
 
-        def Bi(g, h, copy=nc.vector.tensor_copy):
+        def Bi(g, h, copy=nc.vector.tensor_copy, a=0, b=512):
             copy(
-                out=bi[g][h][:].rearrange("p (c i t) -> p c t i", i=4, t=4),
-                in_=eb[g][h][:].rearrange("p t (c i) -> p c t i", i=4),
+                out=bi[g][h][:, 4 * a:4 * b].rearrange("p (c i t) -> p c t i", i=4, t=4),
+                in_=eb[g][h][:, :, a:b].rearrange("p t (c i) -> p c t i", i=4),
             )
 
         def Bq(g, h):
@@ -295,8 +306,8 @@ def tile_neuralsort_ranked_features_s9_kernel(tc, x, w_words, w_scales, gain, sc
                 out=gp[:], in0=nsg[:], scalar=-1.0, in1=vg[:], op0=ALU.mult, op1=ALU.mult)
 
         warm = pb.tile([P, 512], F32, name="pb")
-        for n in range(4):
-            nc.tensor.matmul(warm[:], lhsT=ones[:], rhs=zeros[:], start=True, stop=True)
+        for n in range(32):
+            nc.tensor.matmul(warm[:, 0:128], lhsT=ones[:], rhs=ones[:], start=True, stop=True)
         vectors()
         nc.scalar.activation(out=mlog[:], in_=mant[:].bitcast(F32), func=ACT.Ln)
         nc.vector.tensor_tensor(out=plog[:], in0=mlog[:], in1=elog[:], op=ALU.add)
@@ -305,34 +316,39 @@ def tile_neuralsort_ranked_features_s9_kernel(tc, x, w_words, w_scales, gain, sc
         Xc(0, 0)
         Xq(0, 0)
         T(0, 1)
+        lps = [pa.tile([P, 512], F32, name="pa") for n in range(2)]
+        for n in range(2):
+            nc.tensor.matmul(lps[n][:], lhsT=ones[:], rhs=lrow[:, 512 * n:512 * n + 512], start=True, stop=True)
         Xc(0, 1)
+        for n in range(2):
+            nc.scalar.copy(out=lbc[:, 512 * n:512 * n + 512], in_=lps[n][:])
+        Wsort(0, 2)
         Xq(0, 1)
         for fb in range(4):
             S1(0, 0, fb)
         T(0, 2)
         Xc(0, 2)
         Dv(0, 0)
+        Wsort(0, 3)
         Xq(0, 2)
         for fb in range(4):
             S1(0, 1, fb)
         vectors2()
-        lps = [pa.tile([P, 512], F32, name="pa") for n in range(2)]
-        for n in range(2):
-            nc.tensor.matmul(lps[n][:], lhsT=ones[:], rhs=lrow[:, 512 * n:512 * n + 512], start=True, stop=True)
-        for n in range(2):
-            nc.vector.tensor_copy(out=lbc[:, 512 * n:512 * n + 512], in_=lps[n][:])
         T(0, 3)
         Ds(0, 1)
-        Xc(0, 3)
         Dv(0, 2)
-        Xq(0, 3)
+        Xc(0, 3)
         Ds(0, 3)
+        Wsort(1, 0)
+        Xq(0, 3)
         for fb in range(4):
             S1(0, 2, fb)
         T(1, 0)
         Cb(0)
+        Wsort(1, 1)
         Xc(1, 0)
         E(0, 0, 0)
+        E(0, 0, 1)
         for fb in range(4):
             S1(0, 3, fb)
             Hc(0, fb)
@@ -344,7 +360,6 @@ def tile_neuralsort_ranked_features_s9_kernel(tc, x, w_words, w_scales, gain, sc
                 S1(g, t, fb)
 
         T(1, 1)
-        E(0, 0, 1)
         Xc(1, 1)
         E(0, 0, 2)
         E(0, 0, 3)
@@ -394,33 +409,31 @@ def tile_neuralsort_ranked_features_s9_kernel(tc, x, w_words, w_scales, gain, sc
         Hq(1, 0, 1)
         for t in range(4):
             E(1, 1, t)
+        Bi(1, 1, nc.scalar.copy, 0, 256)
         S1all(1, 4)
         Hc(1, 4)
         S1all(1, 5)
         Hc(1, 5)
         Bi(0, 1)
-        S1all(1, 6)
         for i in range(2):
             S2(i, 0)
             O(i, 0, 1)
+        S1all(1, 6)
         Hc(1, 6)
         Hq(1, 1, 0)
         S1all(1, 7)
-        Bi(1, 1, nc.scalar.copy)
-        Bq(0, 1)
         Hc(1, 7)
         for i in range(2, 4):
             S2(i, 0)
             O(i, 0, 1)
         Hq(1, 1, 1)
+        Bi(1, 1, nc.vector.tensor_copy, 256, 512)
+        Bq(0, 1)
         Bq(1, 1)
 
         for i in range(4):
-            S2t(i, 1)
-            S2g(i, 1, 0)
-        for i in range(4):
-            S2g(i, 1, 1)
-            O(i, 1, i % 2)
+            S2(i, 1)
+            O(i, 1, 0 if i == 2 else 1)
         for i in range(4, 8):
             S2(i, 0)
             O(i, 0, i % 2)

from contextlib import ExitStack

import concourse.mybir as mybir
from concourse.masks import make_identity

FLOPS = 2 * 1024 * 2048 * 1024 + 2 * 1024 * 1024 * 1024

F32 = mybir.dt.float32
BF16 = mybir.dt.bfloat16
I32 = mybir.dt.int32
U32 = mybir.dt.uint32
U8 = mybir.dt.uint8
E4M3 = mybir.dt.float8_e4m3fn_x4
E5M2 = mybir.dt.float8_e5m2_x4
E2M1 = mybir.dt.float4_e2m1fn_x4
ALU = mybir.AluOpType
ACT = mybir.ActivationFunctionType
AXIS = mybir.AxisListType

P = 128
DOCS, K, F, R = 1024, 2048, 1024, 1024
LN2 = 0.6931471805599453


def tile_neuralsort_ranked_features_s9_kernel(tc, x, w_words, w_scales, gain, score, diff, level, prop, out):
    nc = tc.nc
    with ExitStack() as ctx:
        keep = ctx.enter_context(tc.tile_pool(name="keep", bufs=1))
        work = ctx.enter_context(tc.tile_pool(name="work", bufs=3))
        outs = ctx.enter_context(tc.tile_pool(name="outs", bufs=16))
        pa = ctx.enter_context(tc.psum_pool(name="pa", bufs=4))
        pb = ctx.enter_context(tc.psum_pool(name="pb", bufs=4))
        ctx.enter_context(tc.manual_schedule())

        def kt(name, shape, dtype):
            t = keep.tile(shape, dtype, name=name, align_bytes=64)
            return t

        x_view = x.rearrange("(g m t) k -> g t m k", g=2, t=4)
        d_view = diff.rearrange("(g p t) l -> g p t l", g=2, t=4)
        xr = [[kt("xr%d%d" % (g, t), [P, K], BF16) for t in range(4)] for g in range(2)]
        xc = [[kt("xc%d%d" % (g, t), [P, 512], U32) for t in range(4)] for g in range(2)]
        xs = [[kt("xs%d%d" % (g, t), [P, 512], U8) for t in range(4)] for g in range(2)]
        wt = [kt("wt%d" % h, [P, 4, 1024], U8) for h in range(2)]
        ws = [kt("ws%d" % h, [P, 4, 512], U8) for h in range(2)]
        dt = [kt("dt%d" % g, [P, 4, 1024], BF16) for g in range(2)]
        hc = [[kt("hc%d%d" % (g, h), [P, 512], U32) for h in range(2)] for g in range(2)]
        hs = [[kt("hs%d%d" % (g, h), [P, 512], U8) for h in range(2)] for g in range(2)]
        hb = [[kt("hb%d%d" % (g, h), [P, 2048], BF16) for h in range(2)] for g in range(2)]
        bc = [[kt("bc%d%d" % (g, h), [P, 512], U32) for h in range(2)] for g in range(2)]
        bs = [[kt("bs%d%d" % (g, h), [P, 512], U8) for h in range(2)] for g in range(2)]
        eb = [[kt("eb%d%d" % (g, h), [P, 4, 512], BF16) for h in range(2)] for g in range(2)]
        bi = [[kt("bi%d%d" % (g, h), [P, 2048], BF16) for h in range(2)] for g in range(2)]
        ident = kt("ident", [P, P], F32)
        ones = kt("ones", [P, P], BF16)
        one1 = kt("one1", [P, 1], F32)
        dum = kt("dum", [P, 1], F32)
        lrow = kt("lrow", [P, R], BF16)
        lbc = kt("lbc", [P, R], BF16)
        vg = kt("vg", [P, 8], BF16)
        vs = kt("vs", [P, 8], BF16)
        vp = kt("vp", [P, 8], BF16)
        gp = kt("gp", [P, 8], F32)
        s32 = kt("s32", [P, 8], F32)
        p32 = kt("p32", [P, 8], F32)
        expo = kt("expo", [P, 8], I32)
        mant = kt("mant", [P, 8], I32)
        elog = kt("elog", [P, 8], F32)
        mlog = kt("mlog", [P, 8], F32)
        plog = kt("plog", [P, 8], F32)
        pos = kt("pos", [P, 8], F32)
        nsg = kt("nsg", [P, 8], F32)
        rs = kt("rs", [P, 8], F32)
        cb = kt("cb", [P, 8], F32)

        nc.vector.memset(one1[:], 1.0)
        nc.vector.memset(ones[:], 1.0)
        nc.vector.memset(lrow[:].bitcast(I32), 0)
        nc.vector.memset(ws[0][:].bitcast(I32), 0)
        make_identity(nc, ident[:])
        nc.gpsimd.memset(ws[1][:].bitcast(I32), 0)

        ws_view = w_scales.bitcast(I32)
        ww_view = w_words.bitcast(I32)

        def load_scales(eng, h):
            for r in range(4):
                eng.dma_start(
                    out=ws[h][r:P:32, :, :].bitcast(I32),
                    in_=ws_view[:, r:16:4, 128 * h:128 * h + 128].rearrange("c q n -> q c n"),
                )

        def load_x(g, t, h=None):
            cols = slice(0, K) if h is None else slice(1024 * h, 1024 * h + 1024)
            nc.sync.dma_start(out=xr[g][t][:, cols], in_=x_view[g, t][:, cols])

        def load_w(h):
            nc.sync.dma_start(
                out=wt[h][:].bitcast(I32),
                in_=ww_view[:, :, 256 * h:256 * h + 256].rearrange("c p n -> p c n"),
            )

        def load_d(g, half):
            nc.sync.dma_start(out=dt[g][:, 2 * half:2 * half + 2, :], in_=d_view[g][:, 2 * half:2 * half + 2, :])

        def load_vec(eng, v_tile, v):
            eng.dma_start(
                out=v_tile[:].rearrange("p (g t) -> p g t", t=4),
                in_=v.rearrange("(g p t) -> p g t", g=2, t=4),
            )

        load_vec(nc.scalar, vp, prop)
        nc.scalar.dma_start(out=lrow[0:1, :], in_=level.rearrange("(o n) -> o n", o=1))
        load_x(0, 0)
        nc.scalar.activation(out=dum[:], in_=one1[:], func=ACT.Ln)
        load_x(0, 1)
        load_scales(nc.sync, 0)
        load_w(0)
        load_x(0, 2)
        load_vec(nc.sync, vs, score)
        load_vec(nc.sync, vg, gain)
        load_d(0, 0)
        load_x(0, 3)
        load_d(0, 1)
        load_x(1, 0)
        load_x(1, 1)
        load_scales(nc.sync, 1)
        load_w(1)
        load_x(1, 2)
        load_x(1, 3)
        load_d(1, 0)
        load_d(1, 1)

        xg = {}
        banks = {}
        hbank = {}

        sorted_words = {}

        def Wsort(g, t):
            tile = work.tile([P, 1024], F32, name="xw", align_bytes=64)
            sorted_words[g, t] = tile
            for h in range(2):
                w = slice(512 * h, 512 * h + 512)
                nc.vector.tensor_copy(
                    out=tile[:, w].rearrange("p (c u q) -> p c u q", c=2, u=2),
                    in_=xr[g][t][:].bitcast(F32)[:, w].rearrange("p (c q u) -> p c u q", c=2, u=2),
                )

        def T(g, t):
            swd = sorted_words.get((g, t))
            words = xr[g][t][:].bitcast(F32) if swd is None else swd[:]
            for h in range(2):
                ps = pa.tile([P, 512], F32, name="pa")
                banks[g, t, h] = ps
                for c in range(2):
                    for u in range(2):
                        a = 256 * (2 * h + c)
                        nc.tensor.transpose(
                            ps[:, 256 * c + 128 * u:256 * c + 128 * u + 128],
                            words[:, a + u:a + 256:2] if swd is None else words[:, a + 128 * u:a + 128 * u + 128],
                            ident[:],
                        )

        def Xc(g, t):
            tile = work.tile([P, K], BF16, name="xg", align_bytes=64)
            xg[g, t] = tile
            for h in range(2):
                ps = banks[g, t, h]
                nc.scalar.copy(
                    out=tile[:].bitcast(F32)[:, 512 * h:512 * h + 512].rearrange("p (c m u) -> p c m u", c=2, u=2),
                    in_=ps[:].rearrange("p (c u m) -> p c m u", c=2, u=2),
                )

        def Xq(g, t):
            nc.vector.quantize_mx(out=xc[g][t][:].bitcast(E4M3), scales=xs[g][t][:], in_=xg[g, t][:])

        def S1(g, t, fb):
            if (g, fb) not in hbank:
                hps = pb.tile([P, 512], F32, name="pb")
                hbank[g, fb] = hps
            h, b = divmod(fb, 4)
            for c in range(4):
                nc.tensor.matmul_mx(
                    out=hbank[g, fb][:, 128 * t:128 * t + 128],
                    lhsT=xc[g][t][:, 128 * c:128 * c + 128].bitcast(E4M3),
                    lhsT_scale=xs[g][t][:, 128 * c:128 * c + 128],
                    rhs=wt[h][:, c, 256 * b:256 * b + 256].bitcast(E2M1),
                    rhs_scale=ws[h][:, c, 128 * b:128 * b + 128],
                    start=(c == 0),
                    stop=(c == 3),
                )

        def Hc(g, fb):
            h, b = divmod(fb, 4)
            nc.vector.tensor_tensor(
                out=hb[g][h][:, 512 * b:512 * b + 512].rearrange("p (f t) -> p f t", t=4),
                in0=hbank[g, fb][:].rearrange("p (t f) -> p f t", t=4),
                in1=gp[:, 4 * g:4 * g + 4].unsqueeze(1).to_broadcast([P, P, 4]),
                op=ALU.mult,
            )

        def Hq(g, h, half):
            w = slice(256 * half, 256 * half + 256)
            nc.vector.quantize_mx(
                out=hc[g][h][:, w].bitcast(E5M2),
                scales=hs[g][h][:, w],
                in_=hb[g][h][:, 1024 * half:1024 * half + 1024],
            )

        def Dv(g, t):
            nc.vector.tensor_reduce(
                out=rs[:, 4 * g + t:4 * g + t + 1], in_=dt[g][:, t, :], axis=AXIS.X, op=ALU.add,
                apply_absolute_value=True,
            )

        def Ds(g, t):
            junk = work.tile([P, 1024], BF16, name="junk")
            nc.scalar.activation(
                out=junk[:], in_=dt[g][:, t, :], func=ACT.Abs, accum_out=rs[:, 4 * g + t:4 * g + t + 1])

        def Cb(g):
            w = slice(4 * g, 4 * g + 4)
            nc.vector.scalar_tensor_tensor(
                out=cb[:, w], in0=rs[:, w], scalar=-1.0 / 1024.0, in1=plog[:, w], op0=ALU.mult, op1=ALU.add)

        def E(g, h, t):
            j = 4 * g + t
            nc.scalar.activation(
                out=eb[g][h][:, t, :], in_=lbc[:, 512 * h:512 * h + 512], func=ACT.Exp,
                bias=cb[:, j:j + 1], scale=s32[:, j:j + 1])

        def Bi(g, h, copy=nc.vector.tensor_copy, a=0, b=512):
            copy(
                out=bi[g][h][:, 4 * a:4 * b].rearrange("p (c i t) -> p c t i", i=4, t=4),
                in_=eb[g][h][:, :, a:b].rearrange("p t (c i) -> p c t i", i=4),
            )

        def Bq(g, h):
            nc.vector.quantize_mx(out=bc[g][h][:].bitcast(E4M3), scales=bs[g][h][:], in_=bi[g][h][:])

        obank = {}

        def S2g(i, f, g):
            h, b = divmod(i, 4)
            nc.tensor.matmul_mx(
                out=obank[i, f][:],
                lhsT=bc[g][h][:, 128 * b:128 * b + 128].bitcast(E4M3),
                lhsT_scale=bs[g][h][:, 128 * b:128 * b + 128],
                rhs=hc[g][f][:].bitcast(E5M2),
                rhs_scale=hs[g][f][:],
                start=(g == 0),
                stop=(g == 1),
            )

        def S2t(i, f):
            pool, nm = ((pa, "pa"), (pb, "pb"))[f]
            ops = pool.tile([P, 512], F32, name=nm)
            obank[i, f] = ops

        def S2(i, f):
            S2t(i, f)
            S2g(i, f, 0)
            S2g(i, f, 1)

        joined = {}

        def O(i, f, eng):
            if 4 <= i < 7:
                if i not in joined:
                    pair = outs.tile([P, 1024], F32, name="pair", bufs=3)
                    joined[i] = pair
                half = joined[i][:, 512 * f:512 * f + 512]
                if eng == 0:
                    nc.vector.tensor_copy(out=half, in_=obank[i, f][:])
                else:
                    nc.scalar.copy(out=half, in_=obank[i, f][:])
                if f == 1:
                    nc.sync.dma_start(out=out[128 * i:128 * i + 128, :], in_=joined[i][:])
                return
            ot = outs.tile([P, 512], F32, name="ot")
            if eng == 0:
                nc.vector.tensor_copy(out=ot[:], in_=obank[i, f][:])
            else:
                nc.scalar.copy(out=ot[:], in_=obank[i, f][:])
            nc.sync.dma_start(out=out[128 * i:128 * i + 128, 512 * f:512 * f + 512], in_=ot[:])

        def vectors():
            nc.vector.tensor_copy(out=p32[:], in_=vp[:])
            nc.vector.tensor_scalar(
                out=expo[:], in0=p32[:].bitcast(I32), scalar1=23, scalar2=255,
                op0=ALU.logical_shift_right, op1=ALU.bitwise_and)
            nc.vector.tensor_scalar(
                out=mant[:], in0=p32[:].bitcast(I32), scalar1=0x7FFFFF, scalar2=0x3F800000,
                op0=ALU.bitwise_and, op1=ALU.bitwise_or)
            nc.vector.tensor_scalar(
                out=elog[:], in0=expo[:], scalar1=127.0, scalar2=LN2, op0=ALU.subtract, op1=ALU.mult)
            nc.vector.tensor_scalar(
                out=pos[:], in0=p32[:], scalar1=0.0, scalar2=None, op0=ALU.is_gt)
            nc.vector.scalar_tensor_tensor(
                out=nsg[:], in0=p32[:], scalar=0.0, in1=pos[:], op0=ALU.is_lt, op1=ALU.subtract)

        def vectors2():
            nc.vector.tensor_copy(out=s32[:], in_=vs[:])
            nc.vector.scalar_tensor_tensor(
                out=gp[:], in0=nsg[:], scalar=-1.0, in1=vg[:], op0=ALU.mult, op1=ALU.mult)

        warm = pb.tile([P, 512], F32, name="pb")
        for n in range(32):
            nc.tensor.matmul(warm[:, 0:128], lhsT=ones[:], rhs=ones[:], start=True, stop=True)
        vectors()
        nc.scalar.activation(out=mlog[:], in_=mant[:].bitcast(F32), func=ACT.Ln)
        nc.vector.tensor_tensor(out=plog[:], in0=mlog[:], in1=elog[:], op=ALU.add)
        nc.scalar.activation(out=dum[:], in_=one1[:], func=ACT.Exp)
        T(0, 0)
        Xc(0, 0)
        Xq(0, 0)
        T(0, 1)
        lps = [pa.tile([P, 512], F32, name="pa") for n in range(2)]
        for n in range(2):
            nc.tensor.matmul(lps[n][:], lhsT=ones[:], rhs=lrow[:, 512 * n:512 * n + 512], start=True, stop=True)
        Xc(0, 1)
        for n in range(2):
            nc.scalar.copy(out=lbc[:, 512 * n:512 * n + 512], in_=lps[n][:])
        Wsort(0, 2)
        Xq(0, 1)
        for fb in range(4):
            S1(0, 0, fb)
        T(0, 2)
        Xc(0, 2)
        Dv(0, 0)
        Wsort(0, 3)
        Xq(0, 2)
        for fb in range(4):
            S1(0, 1, fb)
        vectors2()
        T(0, 3)
        Ds(0, 1)
        Dv(0, 2)
        Xc(0, 3)
        Ds(0, 3)
        Wsort(1, 0)
        Xq(0, 3)
        for fb in range(4):
            S1(0, 2, fb)
        T(1, 0)
        Cb(0)
        Wsort(1, 1)
        Xc(1, 0)
        E(0, 0, 0)
        E(0, 0, 1)
        for fb in range(4):
            S1(0, 3, fb)
            Hc(0, fb)
            if fb == 1:
                Xq(1, 0)

        def S1all(g, fb):
            for t in range(4):
                S1(g, t, fb)

        T(1, 1)
        Xc(1, 1)
        E(0, 0, 2)
        E(0, 0, 3)
        Hq(0, 0, 0)
        S1all(0, 4)
        Hq(0, 0, 1)
        Xq(1, 1)
        Hc(0, 4)
        T(1, 2)
        Xc(1, 2)
        T(1, 3)
        Xc(1, 3)
        Bi(0, 0)
        S1all(0, 5)
        Xq(1, 2)
        Hc(0, 5)
        Ds(1, 0)
        Hq(0, 1, 0)
        Xq(1, 3)
        Bq(0, 0)
        S1all(0, 6)
        Hc(0, 6)
        Ds(1, 1)
        S1all(0, 7)
        Ds(1, 2)
        Ds(1, 3)
        Hc(0, 7)
        Cb(1)

        E(0, 1, 0)
        S1all(1, 0)
        Hq(0, 1, 1)
        Hc(1, 0)
        for t in range(4):
            E(1, 0, t)
        S1all(1, 1)
        Hc(1, 1)
        for t in range(1, 4):
            E(0, 1, t)
        S1all(1, 2)
        Hq(1, 0, 0)
        Hc(1, 2)
        Bi(1, 0)
        S1all(1, 3)
        Hc(1, 3)
        Bq(1, 0)
        Hq(1, 0, 1)
        for t in range(4):
            E(1, 1, t)
        Bi(1, 1, nc.scalar.copy, 0, 256)
        S1all(1, 4)
        Hc(1, 4)
        S1all(1, 5)
        Hc(1, 5)
        Bi(0, 1)
        for i in range(2):
            S2(i, 0)
            O(i, 0, 1)
        S1all(1, 6)
        Hc(1, 6)
        Hq(1, 1, 0)
        S1all(1, 7)
        Hc(1, 7)
        for i in range(2, 4):
            S2(i, 0)
            O(i, 0, 1)
        Hq(1, 1, 1)
        Bi(1, 1, nc.vector.tensor_copy, 256, 512)
        Bq(0, 1)
        Bq(1, 1)

        for i in range(4):
            S2(i, 1)
            O(i, 1, 0 if i == 2 else 1)
        for i in range(4, 8):
            S2(i, 0)
            O(i, 0, i % 2)
            S2(i, 1)
            O(i, 1, 1 - i % 2)
